import numpy as np
import ml_dtypes


def mxq(x, axis, fmt="e4m3"):
    dtype, down = {"e4m3": (ml_dtypes.float8_e4m3fn, 7), "e5m2": (ml_dtypes.float8_e5m2, 14)}[fmt]
    v = np.moveaxis(np.asarray(x, np.float32).astype(ml_dtypes.bfloat16).astype(np.float64), axis, -1)
    blocks = v.reshape(v.shape[:-1] + (-1, 32))
    amax = np.abs(blocks).max(-1, keepdims=True)
    byte = np.maximum(np.where(amax > 0, np.frexp(amax)[1] - 1 + 127, 0) - down, 1)
    scale = np.exp2(byte - 127.0)
    codes = (blocks / scale).astype(np.float32).astype(dtype).astype(np.float64)
    return np.moveaxis((codes * scale).reshape(v.shape), -1, axis)


WIDE = False


def mx_kscale(k):
    if not WIDE:
        return np.ones(k)
    levels = np.array([10, -10, 5, -5, 0])
    if k % 512:
        return np.exp2(np.random.permutation(np.resize(levels, k // 32))).repeat(32)
    a = np.empty((k // 512, 16))
    for p in range(k // 512):
        a[p, :8] = np.random.permutation(np.resize(levels, 8))
        for g in range(8):
            far = levels[np.abs(levels - a[p, g]) >= 10]
            a[p, g + 8] = far[np.random.randint(len(far))]
    return np.exp2(a.ravel()).repeat(32)


def f64(x):
    return np.asarray(x).astype(np.float64)


def striped(idx):
    return np.tile(idx.reshape(-1, 16).T, (8, 1)).astype(np.uint16)


def unstriped(offs):
    return offs[:16].T.reshape(-1).astype(np.int64)


E2M1 = np.array([0.0, 0.5, 1.0, 1.5, 2.0, 3.0, 4.0, 6.0, -0.0, -0.5, -1.0, -1.5, -2.0, -3.0, -4.0, -6.0])


def pack_weight(w, fmt):
    k, n = w.shape
    w = f64(np.asarray(w, np.float32).astype(ml_dtypes.bfloat16)).reshape(k // 32, 32, n)
    amax = np.abs(w).max(1)
    if fmt == "e4m3":
        byte = np.frexp(amax)[1] - 1 + 127 - 7
    else:
        mant, ex = np.frexp(amax / 6.0)
        byte = np.where(mant > 0.5, ex, ex - 1) + 127
    byte = np.clip(np.where(amax > 0, byte, 1), 1, 254)
    scaled = (w * np.exp2(127.0 - byte)[:, None, :]).reshape(k, n).astype(np.float32)
    by_word = np.ascontiguousarray(scaled.reshape(k // 512, 128, 4, n).transpose(0, 1, 3, 2))
    if fmt == "e4m3":
        words = by_word.astype(ml_dtypes.float8_e4m3fn).view(np.uint8)
    else:
        c = by_word.astype(ml_dtypes.float4_e2m1fn).view(np.uint8) & 0xF
        words = (c[..., 0::2] | (c[..., 1::2] << 4)).reshape(k // 512, 128, 2 * n)
    return np.ascontiguousarray(words), np.ascontiguousarray(byte.astype(np.uint8).reshape(k // 512, 16, n))


def unpack_weight(words, scales, fmt):
    g, _, n = scales.shape
    words = np.ascontiguousarray(words).reshape(g, 128, n, -1)
    if fmt == "e4m3":
        vals = words.view(ml_dtypes.float8_e4m3fn).astype(np.float64)
    else:
        nib = np.empty((g, 128, n, 4), np.uint8)
        nib[..., 0::2] = words & 0xF
        nib[..., 1::2] = words >> 4
        vals = E2M1[nib]
    vals = vals * np.repeat(np.exp2(scales.astype(np.float64) - 127.0), 8, axis=1)[..., None]
    return vals.transpose(0, 1, 3, 2).reshape(g * 512, n)


def silu(v):
    return v / (1.0 + np.exp(-np.maximum(v, -700.0)))


K, M, T, S = 1024, 128, 2048, 1024


def setup_inputs():
    n = np.random.standard_normal
    s = mx_kscale(K)[:, None]
    w = n((K, M)) / np.sqrt(K) / s
    v = pack_weight(n((K, T)) * s, "e4m3")
    p_w4 = pack_weight(w[512:], "e2m1")
    return {
        "tab_words": v[0],
        "tab_scales": v[1],
        "w8": (w[:512]).astype(np.float32),
        "w4_words": p_w4[0],
        "w4_scales": p_w4[1],
        "ts": np.tile(np.exp(0.5 * n(T)), (128, 1)).astype(np.float32),
        "b": (0.3 * n(128)).astype(np.float32),
        "offs": striped(np.random.permutation(T)[:S]),
    }


def reference(tab_words, tab_scales, w8, w4_words, w4_scales, ts, b, offs):
    tab_ = unpack_weight(tab_words, tab_scales, "e4m3")[:, unstriped(offs)]
    w8_ = mxq(f64(w8), 0, "e4m3")
    w4_ = unpack_weight(w4_words, w4_scales, "e2m1")
    y = w8_.T @ tab_[:512] + w4_.T @ tab_[512:]
    y = y * f64(ts)[0][unstriped(offs)]
    return silu(y + f64(b)[:, None])

@@ -1,0 +1,107 @@
+from contextlib import ExitStack
+
+import concourse.mybir as mybir
+from concourse.masks import make_identity
+
+K, M, T, S = 1024, 128, 2048, 1024
+FLOPS = 2 * K * M * S
+
+F32 = mybir.dt.float32
+BF16 = mybir.dt.bfloat16
+I32 = mybir.dt.int32
+U32 = mybir.dt.uint32
+U16 = mybir.dt.uint16
+U8 = mybir.dt.uint8
+FP8X4 = mybir.dt.float8_e4m3fn_x4
+FP4X4 = mybir.dt.float4_e2m1fn_x4
+SILU = mybir.ActivationFunctionType.Silu
+MULT = mybir.AluOpType.mult
+P = 128
+N = 512
+
+
+def tile_list_tabts_silu_kernel(tc, tab_words, tab_scales, w8, w4_words, w4_scales, ts, b, offs, out):
+    nc = tc.nc
+    with ExitStack() as ctx:
+        keep = ctx.enter_context(tc.tile_pool(name="keep", bufs=1))
+        psum = ctx.enter_context(tc.psum_pool(name="psum", bufs=1))
+
+        offsets = keep.tile([P, S // 16], U16, name="offsets")
+        scale_win = keep.tile([P, T // 4], I32, name="scale_win", align_bytes=64)
+        word_win = [keep.tile([P, T], I32, name="word_win%d" % a, align_bytes=64) for a in range(2)]
+        ts_win = keep.tile([P, T], F32, name="ts_win", align_bytes=64)
+        w4_codes = keep.tile([P, 64], I32, name="w4_codes", align_bytes=64)
+        w4_plane = keep.tile([P, 32], I32, name="w4_plane", align_bytes=64)
+        w8_raw = keep.tile([P, 4, M], F32, name="w8_raw", align_bytes=64)
+        w8_bf = keep.tile([P, M, 4], BF16, name="w8_bf", align_bytes=64)
+        w8_codes = keep.tile([P, M], U32, name="w8_codes", align_bytes=64)
+        w8_plane = keep.tile([P, M], U8, name="w8_plane", align_bytes=64)
+        bias = keep.tile([P, 1], F32, name="bias")
+        warm_in = keep.tile([P, 1], F32, name="warm_in")
+        warm_out = keep.tile([P, 1], F32, name="warm_out")
+        got_scales = keep.tile([P, S], U8, name="got_scales", align_bytes=64)
+        got_words = [keep.tile([P, S], U32, name="got_words%d" % a, align_bytes=64) for a in range(2)]
+        y = keep.tile([P, S], F32, name="y", align_bytes=64)
+        scaled = keep.tile([P, S], F32, name="scaled", align_bytes=64)
+        result = keep.tile([P, S], F32, name="result", align_bytes=64)
+        acc = [psum.tile([P, N], F32, name="acc%d" % h) for h in range(2)]
+
+        rows = tab_scales.rearrange("a q t -> (a q) t").bitcast(I32)
+        w4_rows = w4_scales[0].bitcast(I32)
+
+        def words(a):
+            return tab_words[a].rearrange("p t i -> p (t i)").bitcast(I32)
+
+        nc.vector.memset(scale_win[:], 0)
+        nc.sync.dma_start(offsets[:], offs)
+        ts_cols = keep.tile([P, 16], F32, name="ts_cols")
+        nc.sync.dma_start(ts_cols[:], ts[0].rearrange("(n m) -> n m", m=16))
+        for first, row, count in ((12, 0, 32), (68, 0, 32), (0, 16, 4), (44, 4, 4), (64, 24, 4), (108, 12, 4)):
+            nc.sync.dma_start(scale_win[first : first + count, :], rows[row : row + count, :])
+        nc.gpsimd.dma_start(word_win[1][:], words(1))
+        ident = keep.tile([P, P], F32, name="ident")
+        make_identity(nc, ident[:])
+        nc.gpsimd.dma_start(word_win[0][:], words(0))
+        nc.gpsimd.dma_start(w8_raw[:], w8.rearrange("(p j) n -> p j n", j=4))
+        nc.gpsimd.dma_start(w4_codes[:], w4_words[0].bitcast(I32))
+        nc.gpsimd.dma_start(bias[:], b.rearrange("(p o) -> p o", o=1))
+        nc.vector.memset(warm_in[:], 0.0)
+        nc.scalar.activation(warm_out[:], warm_in[:], SILU)
+        nc.vector.memset(w4_plane[:], 0)
+        for quad in range(4):
+            nc.sync.dma_start(w4_plane[32 * quad : 32 * quad + 4, :], w4_rows[4 * quad : 4 * quad + 4, :])
+        for bank in range(4):
+            spread = psum.tile([P, 4, P], F32, name="spread%d" % bank)
+            for i in range(4):
+                m = 4 * bank + i
+                nc.tensor.transpose(spread[:, i, :], ts_cols[:, m : m + 1].to_broadcast([P, P]), ident[:])
+            nc.scalar.copy(ts_win[:].rearrange("p (n c i) -> p c n i", c=4, i=4)[:, bank], spread[:].rearrange("p i n -> p n i"))
+
+        def slots(lo, hi):
+            return offsets[:, lo // 16 : hi // 16]
+
+        def gather_words(a, lo, hi):
+            nc.vector.tensor_copy(got_words[a][:, lo:hi], word_win[a][:].bitcast(U32).indirect(slots(lo, hi)))
+
+        nc.vector.tensor_copy(got_scales[:], scale_win[:].bitcast(U8).indirect(offsets[:]))
+        gather_words(1, 0, S)
+        for h in range(2):
+            cols = slice(h * N, (h + 1) * N)
+            nc.tensor.matmul_mx(
+                acc[h][:], lhsT=w4_codes[:].bitcast(U8).bitcast(FP4X4), lhsT_scale=w4_plane[:].bitcast(U8),
+                rhs=got_words[1][:, cols].bitcast(FP8X4), rhs_scale=got_scales[:, cols], start=True, stop=False)
+        nc.scalar.copy(w8_bf[:], w8_raw[:].rearrange("p j n -> p n j"))
+        gather_words(0, 0, N)
+        nc.vector.quantize_mx(w8_codes[:].bitcast(FP8X4), w8_plane[:], w8_bf[:].rearrange("p n j -> p (n j)"))
+        gather_words(0, N, S)
+        for h in range(2):
+            cols = slice(h * N, (h + 1) * N)
+            nc.tensor.matmul_mx(
+                acc[h][:], lhsT=w8_codes[:].bitcast(FP8X4), lhsT_scale=w8_plane[:],
+                rhs=got_words[0][:, cols].bitcast(FP8X4), rhs_scale=got_scales[12:P, cols], start=False, stop=True)
+            for lo, hi in ((0, 256), (256, 512)):
+                nc.scalar.copy(y[:, h * N + lo : h * N + hi], acc[h][:, lo:hi])
+        for lo, hi in ((0, 512), (512, 768), (768, 896), (896, 1024)):
+            nc.vector.tensor_tensor(scaled[:, lo:hi], ts_win[:].indirect(slots(lo, hi)), y[:, lo:hi], MULT)
+            nc.scalar.activation(result[:, lo:hi], scaled[:, lo:hi], SILU, bias=bias[:])
+            nc.sync.dma_start(out[:, lo:hi], result[:, lo:hi])

@@ -52,24 +52,24 @@ def tile_list_tabts_silu_kernel(tc, tab_words, tab_scales, w8, w4_words, w4_scal
         def words(a):
             return tab_words[a].rearrange("p t i -> p (t i)").bitcast(I32)
 
-        nc.vector.memset(scale_win[:], 0)
         nc.sync.dma_start(offsets[:], offs)
-        ts_cols = keep.tile([P, 16], F32, name="ts_cols")
-        nc.sync.dma_start(ts_cols[:], ts[0].rearrange("(n m) -> n m", m=16))
-        for first, row, count in ((12, 0, 32), (68, 0, 32), (0, 16, 4), (44, 4, 4), (64, 24, 4), (108, 12, 4)):
+        nc.scalar.dma_start(scale_win[100:128, :], rows[4:32, :])
+        for first, row, count in ((12, 0, 32), (68, 0, 32), (44, 4, 16), (60, 20, 8), (0, 16, 12)):
             nc.sync.dma_start(scale_win[first : first + count, :], rows[row : row + count, :])
-        nc.gpsimd.dma_start(word_win[1][:], words(1))
+        nc.sync.dma_start(word_win[1][:], words(1))
         ident = keep.tile([P, P], F32, name="ident")
         make_identity(nc, ident[:])
-        nc.gpsimd.dma_start(word_win[0][:], words(0))
-        nc.gpsimd.dma_start(w8_raw[:], w8.rearrange("(p j) n -> p j n", j=4))
-        nc.gpsimd.dma_start(w4_codes[:], w4_words[0].bitcast(I32))
-        nc.gpsimd.dma_start(bias[:], b.rearrange("(p o) -> p o", o=1))
+        ts_cols = keep.tile([P, 16], F32, name="ts_cols")
+        nc.gpsimd.dma_start(ts_cols[:], ts[0].rearrange("(n m) -> n m", m=16))
+        nc.sync.dma_start(w8_raw[:], w8.rearrange("(p j) n -> p j n", j=4))
+        nc.sync.dma_start(word_win[0][:], words(0))
+        nc.sync.dma_start(w4_codes[:], w4_words[0].bitcast(I32))
         nc.vector.memset(warm_in[:], 0.0)
         nc.scalar.activation(warm_out[:], warm_in[:], SILU)
         nc.vector.memset(w4_plane[:], 0)
         for quad in range(4):
             nc.sync.dma_start(w4_plane[32 * quad : 32 * quad + 4, :], w4_rows[4 * quad : 4 * quad + 4, :])
+        nc.sync.dma_start(bias[:], b.rearrange("(p o) -> p o", o=1))
         for bank in range(4):
             spread = psum.tile([P, 4, P], F32, name="spread%d" % bank)
             for i in range(4):
@@ -101,7 +101,7 @@ def tile_list_tabts_silu_kernel(tc, tab_words, tab_scales, w8, w4_words, w4_scal
                 rhs=got_words[0][:, cols].bitcast(FP8X4), rhs_scale=got_scales[12:P, cols], start=False, stop=True)
             for lo, hi in ((0, 256), (256, 512)):
                 nc.scalar.copy(y[:, h * N + lo : h * N + hi], acc[h][:, lo:hi])
-        for lo, hi in ((0, 512), (512, 768), (768, 896), (896, 1024)):
+        for lo, hi in ((0, 256), (256, 512), (512, 768), (768, 896), (896, 1024)):
             nc.vector.tensor_tensor(scaled[:, lo:hi], ts_win[:].indirect(slots(lo, hi)), y[:, lo:hi], MULT)
             nc.scalar.activation(result[:, lo:hi], scaled[:, lo:hi], SILU, bias=bias[:])
             nc.sync.dma_start(out[:, lo:hi], result[:, lo:hi])

@@ -44,7 +44,7 @@ def tile_list_tabts_silu_kernel(tc, tab_words, tab_scales, w8, w4_words, w4_scal
         y = keep.tile([P, S], F32, name="y", align_bytes=64)
         scaled = keep.tile([P, S], F32, name="scaled", align_bytes=64)
         result = keep.tile([P, S], F32, name="result", align_bytes=64)
-        acc = [psum.tile([P, N], F32, name="acc%d" % h) for h in range(2)]
+        acc = [psum.tile([P, 256], F32, name="acc%d" % h) for h in range(4)]
 
         rows = tab_scales.rearrange("a q t -> (a q) t").bitcast(I32)
         w4_rows = w4_scales[0].bitcast(I32)
@@ -53,22 +53,23 @@ def tile_list_tabts_silu_kernel(tc, tab_words, tab_scales, w8, w4_words, w4_scal
             return tab_words[a].rearrange("p t i -> p (t i)").bitcast(I32)
 
         nc.sync.dma_start(offsets[:], offs)
-        nc.scalar.dma_start(scale_win[100:128, :], rows[4:32, :])
-        for first, row, count in ((12, 0, 32), (68, 0, 32), (44, 4, 16), (60, 20, 8), (0, 16, 12)):
+        for first, row, count in ((100, 4, 28), (44, 4, 16), (60, 20, 8)):
+            nc.scalar.dma_start(scale_win[first : first + count, :], rows[row : row + count, :])
+        for first, row, count in ((12, 0, 32), (68, 0, 32), (0, 16, 12)):
             nc.sync.dma_start(scale_win[first : first + count, :], rows[row : row + count, :])
         nc.sync.dma_start(word_win[1][:], words(1))
         ident = keep.tile([P, P], F32, name="ident")
         make_identity(nc, ident[:])
         ts_cols = keep.tile([P, 16], F32, name="ts_cols")
         nc.gpsimd.dma_start(ts_cols[:], ts[0].rearrange("(n m) -> n m", m=16))
-        nc.sync.dma_start(w8_raw[:], w8.rearrange("(p j) n -> p j n", j=4))
-        nc.sync.dma_start(word_win[0][:], words(0))
-        nc.sync.dma_start(w4_codes[:], w4_words[0].bitcast(I32))
         nc.vector.memset(warm_in[:], 0.0)
         nc.scalar.activation(warm_out[:], warm_in[:], SILU)
         nc.vector.memset(w4_plane[:], 0)
+        nc.sync.dma_start(w8_raw[:], w8.rearrange("(p j) n -> p j n", j=4))
+        nc.sync.dma_start(w4_codes[:], w4_words[0].bitcast(I32))
         for quad in range(4):
             nc.sync.dma_start(w4_plane[32 * quad : 32 * quad + 4, :], w4_rows[4 * quad : 4 * quad + 4, :])
+        nc.sync.dma_start(word_win[0][:], words(0))
         nc.sync.dma_start(bias[:], b.rearrange("(p o) -> p o", o=1))
         for bank in range(4):
             spread = psum.tile([P, 4, P], F32, name="spread%d" % bank)
@@ -85,22 +86,20 @@ def tile_list_tabts_silu_kernel(tc, tab_words, tab_scales, w8, w4_words, w4_scal
 
         nc.vector.tensor_copy(got_scales[:], scale_win[:].bitcast(U8).indirect(offsets[:]))
         gather_words(1, 0, S)
-        for h in range(2):
-            cols = slice(h * N, (h + 1) * N)
-            nc.tensor.matmul_mx(
-                acc[h][:], lhsT=w4_codes[:].bitcast(U8).bitcast(FP4X4), lhsT_scale=w4_plane[:].bitcast(U8),
-                rhs=got_words[1][:, cols].bitcast(FP8X4), rhs_scale=got_scales[:, cols], start=True, stop=False)
         nc.scalar.copy(w8_bf[:], w8_raw[:].rearrange("p j n -> p n j"))
-        gather_words(0, 0, N)
         nc.vector.quantize_mx(w8_codes[:].bitcast(FP8X4), w8_plane[:], w8_bf[:].rearrange("p n j -> p (n j)"))
-        gather_words(0, N, S)
-        for h in range(2):
-            cols = slice(h * N, (h + 1) * N)
-            nc.tensor.matmul_mx(
-                acc[h][:], lhsT=w8_codes[:].bitcast(FP8X4), lhsT_scale=w8_plane[:],
-                rhs=got_words[0][:, cols].bitcast(FP8X4), rhs_scale=got_scales[12:P, cols], start=False, stop=True)
-            for lo, hi in ((0, 256), (256, 512)):
-                nc.scalar.copy(y[:, h * N + lo : h * N + hi], acc[h][:, lo:hi])
+        for h in range(4):
+            gather_words(0, 256 * h, 256 * (h + 1))
+            for g in range(2):
+                cols = slice(256 * h + 128 * g, 256 * h + 128 * (g + 1))
+                part = acc[h][:, 128 * g : 128 * (g + 1)]
+                nc.tensor.matmul_mx(
+                    part, lhsT=w4_codes[:].bitcast(U8).bitcast(FP4X4), lhsT_scale=w4_plane[:].bitcast(U8),
+                    rhs=got_words[1][:, cols].bitcast(FP8X4), rhs_scale=got_scales[:, cols], start=True, stop=False)
+                nc.tensor.matmul_mx(
+                    part, lhsT=w8_codes[:].bitcast(FP8X4), lhsT_scale=w8_plane[:],
+                    rhs=got_words[0][:, cols].bitcast(FP8X4), rhs_scale=got_scales[12:P, cols], start=False, stop=True)
+            nc.scalar.copy(y[:, 256 * h : 256 * (h + 1)], acc[h][:])
         for lo, hi in ((0, 256), (256, 512), (512, 768), (768, 896), (896, 1024)):
             nc.vector.tensor_tensor(scaled[:, lo:hi], ts_win[:].indirect(slots(lo, hi)), y[:, lo:hi], MULT)
             nc.scalar.activation(result[:, lo:hi], scaled[:, lo:hi], SILU, bias=bias[:])

@@ -1,7 +1,6 @@
 from contextlib import ExitStack
 
 import concourse.mybir as mybir
-from concourse.masks import make_identity
 
 K, M, T, S = 1024, 128, 2048, 1024
 FLOPS = 2 * K * M * S
@@ -58,10 +57,6 @@ def tile_list_tabts_silu_kernel(tc, tab_words, tab_scales, w8, w4_words, w4_scal
         for first, row, count in ((12, 0, 32), (68, 0, 32), (0, 16, 12)):
             nc.sync.dma_start(scale_win[first : first + count, :], rows[row : row + count, :])
         nc.sync.dma_start(word_win[1][:], words(1))
-        ident = keep.tile([P, P], F32, name="ident")
-        make_identity(nc, ident[:])
-        ts_cols = keep.tile([P, 16], F32, name="ts_cols")
-        nc.gpsimd.dma_start(ts_cols[:], ts[0].rearrange("(n m) -> n m", m=16))
         nc.vector.memset(warm_in[:], 0.0)
         nc.scalar.activation(warm_out[:], warm_in[:], SILU)
         nc.vector.memset(w4_plane[:], 0)
@@ -70,13 +65,8 @@ def tile_list_tabts_silu_kernel(tc, tab_words, tab_scales, w8, w4_words, w4_scal
         for quad in range(4):
             nc.sync.dma_start(w4_plane[32 * quad : 32 * quad + 4, :], w4_rows[4 * quad : 4 * quad + 4, :])
         nc.sync.dma_start(word_win[0][:], words(0))
+        nc.sync.dma_start(ts_win[:], ts)
         nc.sync.dma_start(bias[:], b.rearrange("(p o) -> p o", o=1))
-        for bank in range(4):
-            spread = psum.tile([P, 4, P], F32, name="spread%d" % bank)
-            for i in range(4):
-                m = 4 * bank + i
-                nc.tensor.transpose(spread[:, i, :], ts_cols[:, m : m + 1].to_broadcast([P, P]), ident[:])
-            nc.scalar.copy(ts_win[:].rearrange("p (n c i) -> p c n i", c=4, i=4)[:, bank], spread[:].rearrange("p i n -> p n i"))
 
         def slots(lo, hi):
             return offsets[:, lo // 16 : hi // 16]

@@ -39,6 +39,7 @@ def tile_list_tabts_silu_kernel(tc, tab_words, tab_scales, w8, w4_words, w4_scal
         warm_in = keep.tile([P, 1], F32, name="warm_in")
         warm_out = keep.tile([P, 1], F32, name="warm_out")
         got_scales = keep.tile([P, S], U8, name="got_scales", align_bytes=64)
+        planes = keep.tile([P, S // 4], I32, name="planes", align_bytes=64)
         got_words = [keep.tile([P, S], U32, name="got_words%d" % a, align_bytes=64) for a in range(2)]
         y = keep.tile([P, S], F32, name="y", align_bytes=64)
         scaled = keep.tile([P, S], F32, name="scaled", align_bytes=64)
@@ -51,22 +52,20 @@ def tile_list_tabts_silu_kernel(tc, tab_words, tab_scales, w8, w4_words, w4_scal
         def words(a):
             return tab_words[a].rearrange("p t i -> p (t i)").bitcast(I32)
 
-        nc.sync.dma_start(offsets[:], offs)
-        for first, row, count in ((100, 4, 28), (44, 4, 16), (60, 20, 8)):
-            nc.scalar.dma_start(scale_win[first : first + count, :], rows[row : row + count, :])
-        for first, row, count in ((12, 0, 32), (68, 0, 32), (0, 16, 12)):
-            nc.sync.dma_start(scale_win[first : first + count, :], rows[row : row + count, :])
-        nc.sync.dma_start(word_win[1][:], words(1))
-        nc.vector.memset(warm_in[:], 0.0)
-        nc.scalar.activation(warm_out[:], warm_in[:], SILU)
         nc.vector.memset(w4_plane[:], 0)
-        nc.sync.dma_start(w8_raw[:], w8.rearrange("(p j) n -> p j n", j=4))
-        nc.sync.dma_start(w4_codes[:], w4_words[0].bitcast(I32))
+        nc.vector.memset(warm_in[:], 0.0)
+        nc.sync.dma_start(offsets[:], offs)
+        nc.scalar.dma_start(scale_win[0:32, :], rows)
+        nc.sync.dma_start(word_win[1][:], words(1))
+        nc.vector.memset(scale_win[32:64, :], 0)
+        nc.vector.memset(scale_win[64:128, :], 0)
+        nc.vector.memset(planes[:], 0)
         for quad in range(4):
-            nc.sync.dma_start(w4_plane[32 * quad : 32 * quad + 4, :], w4_rows[4 * quad : 4 * quad + 4, :])
+            nc.scalar.dma_start(w4_plane[32 * quad : 32 * quad + 4, :], w4_rows[4 * quad : 4 * quad + 4, :])
+        nc.scalar.dma_start(w4_codes[:], w4_words[0].bitcast(I32))
+        nc.scalar.activation(warm_out[:], warm_in[:], SILU)
+        nc.sync.dma_start(w8_raw[:], w8.rearrange("(p j) n -> p j n", j=4))
         nc.sync.dma_start(word_win[0][:], words(0))
-        nc.sync.dma_start(ts_win[:], ts)
-        nc.sync.dma_start(bias[:], b.rearrange("(p o) -> p o", o=1))
 
         def slots(lo, hi):
             return offsets[:, lo // 16 : hi // 16]
@@ -75,6 +74,10 @@ def tile_list_tabts_silu_kernel(tc, tab_words, tab_scales, w8, w4_words, w4_scal
             nc.vector.tensor_copy(got_words[a][:, lo:hi], word_win[a][:].bitcast(U32).indirect(slots(lo, hi)))
 
         nc.vector.tensor_copy(got_scales[:], scale_win[:].bitcast(U8).indirect(offsets[:]))
+        for first, row, count in ((0, 16, 4), (12, 0, 32), (44, 4, 32), (76, 8, 32), (108, 12, 4)):
+            nc.sync.dma_start(planes[first : first + count, :], got_scales[row : row + count, :].bitcast(I32))
+        nc.sync.dma_start(ts_win[:], ts)
+        nc.sync.dma_start(bias[:], b.rearrange("(p o) -> p o", o=1))
         gather_words(1, 0, S)
         nc.scalar.copy(w8_bf[:], w8_raw[:].rearrange("p j n -> p n j"))
         nc.vector.quantize_mx(w8_codes[:].bitcast(FP8X4), w8_plane[:], w8_bf[:].rearrange("p n j -> p (n j)"))
@@ -85,10 +88,10 @@ def tile_list_tabts_silu_kernel(tc, tab_words, tab_scales, w8, w4_words, w4_scal
                 part = acc[h][:, 128 * g : 128 * (g + 1)]
                 nc.tensor.matmul_mx(
                     part, lhsT=w4_codes[:].bitcast(U8).bitcast(FP4X4), lhsT_scale=w4_plane[:].bitcast(U8),
-                    rhs=got_words[1][:, cols].bitcast(FP8X4), rhs_scale=got_scales[:, cols], start=True, stop=False)
+                    rhs=got_words[1][:, cols].bitcast(FP8X4), rhs_scale=planes[:].bitcast(U8)[:, cols], start=True, stop=False)
                 nc.tensor.matmul_mx(
                     part, lhsT=w8_codes[:].bitcast(FP8X4), lhsT_scale=w8_plane[:],
-                    rhs=got_words[0][:, cols].bitcast(FP8X4), rhs_scale=got_scales[12:P, cols], start=False, stop=True)
+                    rhs=got_words[0][:, cols].bitcast(FP8X4), rhs_scale=planes[:].bitcast(U8)[12:P, cols], start=False, stop=True)
             nc.scalar.copy(y[:, 256 * h : 256 * (h + 1)], acc[h][:])
         for lo, hi in ((0, 256), (256, 512), (512, 768), (768, 896), (896, 1024)):
             nc.vector.tensor_tensor(scaled[:, lo:hi], ts_win[:].indirect(slots(lo, hi)), y[:, lo:hi], MULT)

@@ -1,6 +1,7 @@
 from contextlib import ExitStack
 
 import concourse.mybir as mybir
+from concourse.masks import make_identity
 
 K, M, T, S = 1024, 128, 2048, 1024
 FLOPS = 2 * K * M * S
@@ -29,6 +30,8 @@ def tile_list_tabts_silu_kernel(tc, tab_words, tab_scales, w8, w4_words, w4_scal
         scale_win = keep.tile([P, T // 4], I32, name="scale_win", align_bytes=64)
         word_win = [keep.tile([P, T], I32, name="word_win%d" % a, align_bytes=64) for a in range(2)]
         ts_win = keep.tile([P, T], F32, name="ts_win", align_bytes=64)
+        ts_cols = keep.tile([P, 16], F32, name="ts_cols", align_bytes=64)
+        ident = keep.tile([P, P], F32, name="ident", align_bytes=64)
         w4_codes = keep.tile([P, 64], I32, name="w4_codes", align_bytes=64)
         w4_plane = keep.tile([P, 32], I32, name="w4_plane", align_bytes=64)
         w8_raw = keep.tile([P, 4, M], F32, name="w8_raw", align_bytes=64)
@@ -40,11 +43,13 @@ def tile_list_tabts_silu_kernel(tc, tab_words, tab_scales, w8, w4_words, w4_scal
         warm_out = keep.tile([P, 1], F32, name="warm_out")
         got_scales = keep.tile([P, S], U8, name="got_scales", align_bytes=64)
         planes = keep.tile([P, S // 4], I32, name="planes", align_bytes=64)
-        got_words = [keep.tile([P, S], U32, name="got_words%d" % a, align_bytes=64) for a in range(2)]
+        got_words1 = keep.tile([P, S], U32, name="got_words1", align_bytes=64)
         y = keep.tile([P, S], F32, name="y", align_bytes=64)
         scaled = keep.tile([P, S], F32, name="scaled", align_bytes=64)
         result = keep.tile([P, S], F32, name="result", align_bytes=64)
         acc = [psum.tile([P, 256], F32, name="acc%d" % h) for h in range(4)]
+
+        spread = [psum.tile([P, 4, P], F32, name="spread%d" % h) for h in range(4)]
 
         rows = tab_scales.rearrange("a q t -> (a q) t").bitcast(I32)
         w4_rows = w4_scales[0].bitcast(I32)
@@ -57,42 +62,53 @@ def tile_list_tabts_silu_kernel(tc, tab_words, tab_scales, w8, w4_words, w4_scal
         nc.sync.dma_start(offsets[:], offs)
         nc.scalar.dma_start(scale_win[0:32, :], rows)
         nc.sync.dma_start(word_win[1][:], words(1))
+        nc.scalar.dma_start(ts_cols[:], ts[0].rearrange("(p c) -> p c", c=16))
+        make_identity(nc, ident[:])
         nc.vector.memset(scale_win[32:64, :], 0)
         nc.vector.memset(scale_win[64:128, :], 0)
         nc.vector.memset(planes[:], 0)
         for quad in range(4):
             nc.scalar.dma_start(w4_plane[32 * quad : 32 * quad + 4, :], w4_rows[4 * quad : 4 * quad + 4, :])
-        nc.scalar.dma_start(w4_codes[:], w4_words[0].bitcast(I32))
         nc.scalar.activation(warm_out[:], warm_in[:], SILU)
         nc.sync.dma_start(w8_raw[:], w8.rearrange("(p j) n -> p j n", j=4))
         nc.sync.dma_start(word_win[0][:], words(0))
+        nc.sync.dma_start(w4_codes[:], w4_words[0].bitcast(I32))
+        for quarter in range(4):
+            for c in range(4):
+                col = 4 * quarter + c
+                nc.tensor.transpose(spread[quarter][:, c, :], ts_cols[:, col : col + 1].to_broadcast([P, P]), ident[:])
+            nc.scalar.copy(
+                ts_win[:].rearrange("q (p c) -> q p c", c=16)[:, :, 4 * quarter : 4 * quarter + 4],
+                spread[quarter][:].rearrange("q c p -> q p c"))
 
         def slots(lo, hi):
             return offsets[:, lo // 16 : hi // 16]
 
-        def gather_words(a, lo, hi):
-            nc.vector.tensor_copy(got_words[a][:, lo:hi], word_win[a][:].bitcast(U32).indirect(slots(lo, hi)))
+        def gather_words(dst, a, lo, hi):
+            nc.vector.tensor_copy(dst, word_win[a][:].bitcast(U32).indirect(slots(lo, hi)))
 
         nc.vector.tensor_copy(got_scales[:], scale_win[:].bitcast(U8).indirect(offsets[:]))
         for first, row, count in ((0, 16, 4), (12, 0, 32), (44, 4, 32), (76, 8, 32), (108, 12, 4)):
             nc.sync.dma_start(planes[first : first + count, :], got_scales[row : row + count, :].bitcast(I32))
-        nc.sync.dma_start(ts_win[:], ts)
         nc.sync.dma_start(bias[:], b.rearrange("(p o) -> p o", o=1))
-        gather_words(1, 0, S)
+        gather_words(got_words1[:], 1, 0, S)
+        plane_bytes = planes[:].bitcast(U8)
+        for g in range(8):
+            cols = slice(128 * g, 128 * (g + 1))
+            nc.tensor.matmul_mx(
+                acc[g // 2][:, 128 * (g % 2) : 128 * (g % 2 + 1)],
+                lhsT=w4_codes[:].bitcast(U8).bitcast(FP4X4), lhsT_scale=w4_plane[:].bitcast(U8),
+                rhs=got_words1[:, cols].bitcast(FP8X4), rhs_scale=plane_bytes[:, cols], start=(g % 2 == 0), stop=False)
         nc.scalar.copy(w8_bf[:], w8_raw[:].rearrange("p j n -> p n j"))
         nc.vector.quantize_mx(w8_codes[:].bitcast(FP8X4), w8_plane[:], w8_bf[:].rearrange("p n j -> p (n j)"))
         for h in range(4):
-            gather_words(0, 256 * h, 256 * (h + 1))
-            for g in range(2):
-                cols = slice(256 * h + 128 * g, 256 * h + 128 * (g + 1))
-                part = acc[h][:, 128 * g : 128 * (g + 1)]
-                nc.tensor.matmul_mx(
-                    part, lhsT=w4_codes[:].bitcast(U8).bitcast(FP4X4), lhsT_scale=w4_plane[:].bitcast(U8),
-                    rhs=got_words[1][:, cols].bitcast(FP8X4), rhs_scale=planes[:].bitcast(U8)[:, cols], start=True, stop=False)
-                nc.tensor.matmul_mx(
-                    part, lhsT=w8_codes[:].bitcast(FP8X4), lhsT_scale=w8_plane[:],
-                    rhs=got_words[0][:, cols].bitcast(FP8X4), rhs_scale=planes[:].bitcast(U8)[12:P, cols], start=False, stop=True)
-            nc.scalar.copy(y[:, 256 * h : 256 * (h + 1)], acc[h][:])
+            got = keep.tile([P, 256], U32, name="got_words0_%d" % h, align_bytes=64)
+            cols = slice(256 * h, 256 * (h + 1))
+            gather_words(got[:], 0, 256 * h, 256 * (h + 1))
+            nc.tensor.matmul_mx(
+                acc[h][:], lhsT=w8_codes[:].bitcast(FP8X4), lhsT_scale=w8_plane[:],
+                rhs=got[:].bitcast(FP8X4), rhs_scale=plane_bytes[12:P, cols], start=False, stop=True)
+            nc.scalar.copy(y[:, cols], acc[h][:])
         for lo, hi in ((0, 256), (256, 512), (512, 768), (768, 896), (896, 1024)):
             nc.vector.tensor_tensor(scaled[:, lo:hi], ts_win[:].indirect(slots(lo, hi)), y[:, lo:hi], MULT)
             nc.scalar.activation(result[:, lo:hi], scaled[:, lo:hi], SILU, bias=bias[:])

@@ -93,18 +93,18 @@ def tile_list_tabts_silu_kernel(tc, tab_words, tab_scales, w8, w4_words, w4_scal
         nc.sync.dma_start(bias[:], b.rearrange("(p o) -> p o", o=1))
         gather_words(got_words1[:], 1, 0, S)
         plane_bytes = planes[:].bitcast(U8)
-        for g in range(8):
-            cols = slice(128 * g, 128 * (g + 1))
-            nc.tensor.matmul_mx(
-                acc[g // 2][:, 128 * (g % 2) : 128 * (g % 2 + 1)],
-                lhsT=w4_codes[:].bitcast(U8).bitcast(FP4X4), lhsT_scale=w4_plane[:].bitcast(U8),
-                rhs=got_words1[:, cols].bitcast(FP8X4), rhs_scale=plane_bytes[:, cols], start=(g % 2 == 0), stop=False)
         nc.scalar.copy(w8_bf[:], w8_raw[:].rearrange("p j n -> p n j"))
         nc.vector.quantize_mx(w8_codes[:].bitcast(FP8X4), w8_plane[:], w8_bf[:].rearrange("p n j -> p (n j)"))
         for h in range(4):
             got = keep.tile([P, 256], U32, name="got_words0_%d" % h, align_bytes=64)
             cols = slice(256 * h, 256 * (h + 1))
             gather_words(got[:], 0, 256 * h, 256 * (h + 1))
+            for g in range(2):
+                half = slice(256 * h + 128 * g, 256 * h + 128 * (g + 1))
+                nc.tensor.matmul_mx(
+                    acc[h][:, 128 * g : 128 * (g + 1)],
+                    lhsT=w4_codes[:].bitcast(U8).bitcast(FP4X4), lhsT_scale=w4_plane[:].bitcast(U8),
+                    rhs=got_words1[:, half].bitcast(FP8X4), rhs_scale=plane_bytes[:, half], start=(g == 0), stop=False)
             nc.tensor.matmul_mx(
                 acc[h][:], lhsT=w8_codes[:].bitcast(FP8X4), lhsT_scale=w8_plane[:],
                 rhs=got[:].bitcast(FP8X4), rhs_scale=plane_bytes[12:P, cols], start=False, stop=True)

@@ -63,10 +63,10 @@ def tile_list_tabts_silu_kernel(tc, tab_words, tab_scales, w8, w4_words, w4_scal
         nc.scalar.dma_start(scale_win[0:32, :], rows)
         nc.sync.dma_start(word_win[1][:], words(1))
         nc.scalar.dma_start(ts_cols[:], ts[0].rearrange("(p c) -> p c", c=16))
-        make_identity(nc, ident[:])
-        nc.vector.memset(scale_win[32:64, :], 0)
+        nc.gpsimd.memset(scale_win[32:64, :], 0)
         nc.vector.memset(scale_win[64:128, :], 0)
-        nc.vector.memset(planes[:], 0)
+        make_identity(nc, ident[:])
+        nc.gpsimd.memset(planes[:], 0)
         for quad in range(4):
             nc.scalar.dma_start(w4_plane[32 * quad : 32 * quad + 4, :], w4_rows[4 * quad : 4 * quad + 4, :])
         nc.scalar.activation(warm_out[:], warm_in[:], SILU)

@@ -33,7 +33,6 @@ def tile_list_tabts_silu_kernel(tc, tab_words, tab_scales, w8, w4_words, w4_scal
         ts_cols = keep.tile([P, 16], F32, name="ts_cols", align_bytes=64)
         ident = keep.tile([P, P], F32, name="ident", align_bytes=64)
         w4_codes = keep.tile([P, 64], I32, name="w4_codes", align_bytes=64)
-        w4_plane = keep.tile([P, 32], I32, name="w4_plane", align_bytes=64)
         w8_raw = keep.tile([P, 4, M], F32, name="w8_raw", align_bytes=64)
         w8_bf = keep.tile([P, M, 4], BF16, name="w8_bf", align_bytes=64)
         w8_codes = keep.tile([P, M], U32, name="w8_codes", align_bytes=64)
@@ -42,7 +41,8 @@ def tile_list_tabts_silu_kernel(tc, tab_words, tab_scales, w8, w4_words, w4_scal
         warm_in = keep.tile([P, 1], F32, name="warm_in")
         warm_out = keep.tile([P, 1], F32, name="warm_out")
         got_scales = keep.tile([P, S], U8, name="got_scales", align_bytes=64)
-        planes = keep.tile([P, S // 4], I32, name="planes", align_bytes=64)
+        planes = keep.tile([P, S // 4 + 32], I32, name="planes", align_bytes=64)
+        w4_plane = planes[:, S // 4 :]
         got_words1 = keep.tile([P, S], U32, name="got_words1", align_bytes=64)
         y = keep.tile([P, S], F32, name="y", align_bytes=64)
         scaled = keep.tile([P, S], F32, name="scaled", align_bytes=64)
@@ -57,18 +57,17 @@ def tile_list_tabts_silu_kernel(tc, tab_words, tab_scales, w8, w4_words, w4_scal
         def words(a):
             return tab_words[a].rearrange("p t i -> p (t i)").bitcast(I32)
 
-        nc.vector.memset(w4_plane[:], 0)
+        nc.vector.memset(ident[:], 0.0)
+        nc.vector.memset(planes[:], 0)
         nc.vector.memset(warm_in[:], 0.0)
+        nc.vector.memset(scale_win[0:96, :], 0)
         nc.sync.dma_start(offsets[:], offs)
-        nc.scalar.dma_start(scale_win[0:32, :], rows)
+        nc.scalar.dma_start(scale_win[96:128, :], rows)
         nc.sync.dma_start(word_win[1][:], words(1))
         nc.scalar.dma_start(ts_cols[:], ts[0].rearrange("(p c) -> p c", c=16))
-        nc.gpsimd.memset(scale_win[32:64, :], 0)
-        nc.vector.memset(scale_win[64:128, :], 0)
-        make_identity(nc, ident[:])
-        nc.gpsimd.memset(planes[:], 0)
+        make_identity(nc, ident[:], nomemset=True)
         for quad in range(4):
-            nc.scalar.dma_start(w4_plane[32 * quad : 32 * quad + 4, :], w4_rows[4 * quad : 4 * quad + 4, :])
+            nc.scalar.dma_start(planes[32 * quad : 32 * quad + 4, S // 4 :], w4_rows[4 * quad : 4 * quad + 4, :])
         nc.scalar.activation(warm_out[:], warm_in[:], SILU)
         nc.sync.dma_start(w8_raw[:], w8.rearrange("(p j) n -> p j n", j=4))
         nc.sync.dma_start(word_win[0][:], words(0))
@@ -88,8 +87,8 @@ def tile_list_tabts_silu_kernel(tc, tab_words, tab_scales, w8, w4_words, w4_scal
             nc.vector.tensor_copy(dst, word_win[a][:].bitcast(U32).indirect(slots(lo, hi)))
 
         nc.vector.tensor_copy(got_scales[:], scale_win[:].bitcast(U8).indirect(offsets[:]))
-        for first, row, count in ((0, 16, 4), (12, 0, 32), (44, 4, 32), (76, 8, 32), (108, 12, 4)):
-            nc.sync.dma_start(planes[first : first + count, :], got_scales[row : row + count, :].bitcast(I32))
+        for first, row, count in ((0, 112, 4), (4, 88, 32), (36, 92, 32), (68, 96, 32), (108, 108, 4)):
+            nc.sync.dma_start(planes[first : first + count, 0 : S // 4], got_scales[row : row + count, :].bitcast(I32))
         nc.sync.dma_start(bias[:], b.rearrange("(p o) -> p o", o=1))
         gather_words(got_words1[:], 1, 0, S)
         plane_bytes = planes[:].bitcast(U8)
@@ -103,7 +102,7 @@ def tile_list_tabts_silu_kernel(tc, tab_words, tab_scales, w8, w4_words, w4_scal
                 half = slice(256 * h + 128 * g, 256 * h + 128 * (g + 1))
                 nc.tensor.matmul_mx(
                     acc[h][:, 128 * g : 128 * (g + 1)],
-                    lhsT=w4_codes[:].bitcast(U8).bitcast(FP4X4), lhsT_scale=w4_plane[:].bitcast(U8),
+                    lhsT=w4_codes[:].bitcast(U8).bitcast(FP4X4), lhsT_scale=w4_plane.bitcast(U8),
                     rhs=got_words1[:, half].bitcast(FP8X4), rhs_scale=plane_bytes[:, half], start=(g == 0), stop=False)
             nc.tensor.matmul_mx(
                 acc[h][:], lhsT=w8_codes[:].bitcast(FP8X4), lhsT_scale=w8_plane[:],

@@ -24,16 +24,17 @@ def tile_list_tabts_silu_kernel(tc, tab_words, tab_scales, w8, w4_words, w4_scal
     nc = tc.nc
     with ExitStack() as ctx:
         keep = ctx.enter_context(tc.tile_pool(name="keep", bufs=1))
+        far = ctx.enter_context(tc.tile_pool(name="far", bufs=1))
         psum = ctx.enter_context(tc.psum_pool(name="psum", bufs=1))
 
         offsets = keep.tile([P, S // 16], U16, name="offsets")
-        scale_win = keep.tile([P, T // 4], I32, name="scale_win", align_bytes=64)
-        word_win = [keep.tile([P, T], I32, name="word_win%d" % a, align_bytes=64) for a in range(2)]
-        ts_win = keep.tile([P, T], F32, name="ts_win", align_bytes=64)
+        scale_win = far.tile([P, T // 4], I32, name="scale_win", align_bytes=64, offset=46 * 1024)
+        word_win = [far.tile([P, T], I32, name="word_win%d" % a, align_bytes=64, offset=(50 + 60 * a) * 1024) for a in range(2)]
+        ts_win = far.tile([P, T], F32, name="ts_win", align_bytes=64, offset=174 * 1024)
         ts_cols = keep.tile([P, 16], F32, name="ts_cols", align_bytes=64)
         ident = keep.tile([P, P], F32, name="ident", align_bytes=64)
         w4_codes = keep.tile([P, 64], I32, name="w4_codes", align_bytes=64)
-        w8_raw = keep.tile([P, 4, M], F32, name="w8_raw", align_bytes=64)
+        w8_raw = far.tile([P, 4, M], F32, name="w8_raw", align_bytes=64, offset=184 * 1024)
         w8_bf = keep.tile([P, M, 4], BF16, name="w8_bf", align_bytes=64)
         w8_codes = keep.tile([P, M], U32, name="w8_codes", align_bytes=64)
         w8_plane = keep.tile([P, M], U8, name="w8_plane", align_bytes=64)
@@ -45,8 +46,8 @@ def tile_list_tabts_silu_kernel(tc, tab_words, tab_scales, w8, w4_words, w4_scal
         w4_plane = planes[:, S // 4 :]
         got_words1 = keep.tile([P, S], U32, name="got_words1", align_bytes=64)
         y = keep.tile([P, S], F32, name="y", align_bytes=64)
-        scaled = keep.tile([P, S], F32, name="scaled", align_bytes=64)
-        result = keep.tile([P, S], F32, name="result", align_bytes=64)
+        scaled = far.tile([P, S], F32, name="scaled", align_bytes=64, offset=120 * 1024)
+        result = far.tile([P, S], F32, name="result", align_bytes=64, offset=60 * 1024)
         acc = [psum.tile([P, 256], F32, name="acc%d" % h) for h in range(4)]
 
         spread = [psum.tile([P, 4, P], F32, name="spread%d" % h) for h in range(4)]

@@ -28,13 +28,13 @@ def tile_list_tabts_silu_kernel(tc, tab_words, tab_scales, w8, w4_words, w4_scal
         psum = ctx.enter_context(tc.psum_pool(name="psum", bufs=1))
 
         offsets = keep.tile([P, S // 16], U16, name="offsets")
-        scale_win = far.tile([P, T // 4], I32, name="scale_win", align_bytes=64, offset=46 * 1024)
-        word_win = [far.tile([P, T], I32, name="word_win%d" % a, align_bytes=64, offset=(50 + 60 * a) * 1024) for a in range(2)]
-        ts_win = far.tile([P, T], F32, name="ts_win", align_bytes=64, offset=174 * 1024)
+        scale_win = far.tile([P, T // 4], I32, name="scale_win", align_bytes=64, offset=62 * 1024)
+        word_win = [far.tile([P, T], I32, name="word_win%d" % a, align_bytes=64, offset=(54 + 56 * a) * 1024) for a in range(2)]
+        ts_win = far.tile([P, T], F32, name="ts_win", align_bytes=64, offset=190 * 1024)
         ts_cols = keep.tile([P, 16], F32, name="ts_cols", align_bytes=64)
         ident = keep.tile([P, P], F32, name="ident", align_bytes=64)
         w4_codes = keep.tile([P, 64], I32, name="w4_codes", align_bytes=64)
-        w8_raw = far.tile([P, 4, M], F32, name="w8_raw", align_bytes=64, offset=184 * 1024)
+        w8_raw = far.tile([P, 4, M], F32, name="w8_raw", align_bytes=64, offset=174 * 1024)
         w8_bf = keep.tile([P, M, 4], BF16, name="w8_bf", align_bytes=64)
         w8_codes = keep.tile([P, M], U32, name="w8_codes", align_bytes=64)
         w8_plane = keep.tile([P, M], U8, name="w8_plane", align_bytes=64)
@@ -46,8 +46,8 @@ def tile_list_tabts_silu_kernel(tc, tab_words, tab_scales, w8, w4_words, w4_scal
         w4_plane = planes[:, S // 4 :]
         got_words1 = keep.tile([P, S], U32, name="got_words1", align_bytes=64)
         y = keep.tile([P, S], F32, name="y", align_bytes=64)
-        scaled = far.tile([P, S], F32, name="scaled", align_bytes=64, offset=120 * 1024)
-        result = far.tile([P, S], F32, name="result", align_bytes=64, offset=60 * 1024)
+        scaled = far.tile([P, S], F32, name="scaled", align_bytes=64, offset=118 * 1024)
+        result = far.tile([P, S], F32, name="result", align_bytes=64, offset=46 * 1024)
         acc = [psum.tile([P, 256], F32, name="acc%d" % h) for h in range(4)]
 
         spread = [psum.tile([P, 4, P], F32, name="spread%d" % h) for h in range(4)]

@@ -16,8 +16,36 @@ FP8X4 = mybir.dt.float8_e4m3fn_x4
 FP4X4 = mybir.dt.float4_e2m1fn_x4
 SILU = mybir.ActivationFunctionType.Silu
 MULT = mybir.AluOpType.mult
+
 P = 128
-N = 512
+QUAD = 32
+LIST_ROWS = 16
+BLOCKS = 16
+PLANE_WORDS = S // 4
+W4_PLANE_WORDS = M // 4
+
+SCALE_ROW0 = P - 2 * BLOCKS
+PASS0_FIRST = 12
+
+BANK = 256
+E2M1_COLS = 128
+SLICES = [(lo, lo + BANK) for lo in range(0, S - BANK, BANK)] + [(S - BANK, S - BANK // 2), (S - BANK // 2, S)]
+
+TS_COLS = T // P
+TURNS = 4
+
+
+def place(stretch, lane):
+    return (46 + 64 * stretch + 8 * lane) * 1024
+
+
+def plane_moves():
+    moves = [(0, SCALE_ROW0 + BLOCKS, 4)]
+    for quad in range(3):
+        first = QUAD * quad + 4
+        moves.append((first, SCALE_ROW0 + 4 * quad - (PASS0_FIRST - 4), QUAD))
+    moves.append((QUAD * 3 + PASS0_FIRST, SCALE_ROW0 + 4 * 3, 4))
+    return moves
 
 
 def tile_list_tabts_silu_kernel(tc, tab_words, tab_scales, w8, w4_words, w4_scales, ts, b, offs, out):
@@ -27,14 +55,14 @@ def tile_list_tabts_silu_kernel(tc, tab_words, tab_scales, w8, w4_words, w4_scal
         far = ctx.enter_context(tc.tile_pool(name="far", bufs=1))
         psum = ctx.enter_context(tc.psum_pool(name="psum", bufs=1))
 
-        offsets = keep.tile([P, S // 16], U16, name="offsets")
-        scale_win = far.tile([P, T // 4], I32, name="scale_win", align_bytes=64, offset=62 * 1024)
-        word_win = [far.tile([P, T], I32, name="word_win%d" % a, align_bytes=64, offset=(54 + 56 * a) * 1024) for a in range(2)]
-        ts_win = far.tile([P, T], F32, name="ts_win", align_bytes=64, offset=190 * 1024)
-        ts_cols = keep.tile([P, 16], F32, name="ts_cols", align_bytes=64)
+        offsets = keep.tile([P, S // LIST_ROWS], U16, name="offsets")
+        scale_win = far.tile([P, T // 4], I32, name="scale_win", align_bytes=64, offset=place(0, 2))
+        word_win = [far.tile([P, T], I32, name="word_win%d" % a, align_bytes=64, offset=place(a, 1 - a)) for a in range(2)]
+        ts_win = far.tile([P, T], F32, name="ts_win", align_bytes=64, offset=place(2, 2))
+        ts_cols = keep.tile([P, TS_COLS], F32, name="ts_cols", align_bytes=64)
         ident = keep.tile([P, P], F32, name="ident", align_bytes=64)
-        w4_codes = keep.tile([P, 64], I32, name="w4_codes", align_bytes=64)
-        w8_raw = far.tile([P, 4, M], F32, name="w8_raw", align_bytes=64, offset=174 * 1024)
+        w4_codes = keep.tile([P, 2 * M // 4], I32, name="w4_codes", align_bytes=64)
+        w8_raw = far.tile([P, 4, M], F32, name="w8_raw", align_bytes=64, offset=place(2, 0))
         w8_bf = keep.tile([P, M, 4], BF16, name="w8_bf", align_bytes=64)
         w8_codes = keep.tile([P, M], U32, name="w8_codes", align_bytes=64)
         w8_plane = keep.tile([P, M], U8, name="w8_plane", align_bytes=64)
@@ -42,74 +70,74 @@ def tile_list_tabts_silu_kernel(tc, tab_words, tab_scales, w8, w4_words, w4_scal
         warm_in = keep.tile([P, 1], F32, name="warm_in")
         warm_out = keep.tile([P, 1], F32, name="warm_out")
         got_scales = keep.tile([P, S], U8, name="got_scales", align_bytes=64)
-        planes = keep.tile([P, S // 4 + 32], I32, name="planes", align_bytes=64)
-        w4_plane = planes[:, S // 4 :]
+        plane_tile = keep.tile([P, PLANE_WORDS + W4_PLANE_WORDS], I32, name="planes", align_bytes=64)
+        table_planes = plane_tile[:, 0:PLANE_WORDS]
+        w4_plane = plane_tile[:, PLANE_WORDS:]
         got_words1 = keep.tile([P, S], U32, name="got_words1", align_bytes=64)
-        y = keep.tile([P, S], F32, name="y", align_bytes=64)
-        scaled = far.tile([P, S], F32, name="scaled", align_bytes=64, offset=118 * 1024)
-        result = far.tile([P, S], F32, name="result", align_bytes=64, offset=46 * 1024)
-        acc = [psum.tile([P, 256], F32, name="acc%d" % h) for h in range(4)]
-
-        spread = [psum.tile([P, 4, P], F32, name="spread%d" % h) for h in range(4)]
-
-        rows = tab_scales.rearrange("a q t -> (a q) t").bitcast(I32)
-        w4_rows = w4_scales[0].bitcast(I32)
+        sums = keep.tile([P, S], F32, name="y", align_bytes=64)
+        scaled = far.tile([P, S], F32, name="scaled", align_bytes=64, offset=place(1, 1))
+        result = far.tile([P, S], F32, name="result", align_bytes=64, offset=place(0, 0))
+        acc = [psum.tile([P, BANK], F32, name="acc%d" % h) for h in range(S // BANK)]
+        spread = [psum.tile([P, TURNS, P], F32, name="spread%d" % h) for h in range(TS_COLS // TURNS)]
 
         def words(a):
             return tab_words[a].rearrange("p t i -> p (t i)").bitcast(I32)
 
+        def entries(lo, hi):
+            return offsets[:, lo // LIST_ROWS : hi // LIST_ROWS]
+
         nc.vector.memset(ident[:], 0.0)
-        nc.vector.memset(planes[:], 0)
+        nc.vector.memset(w4_plane, 0)
+        nc.vector.memset(table_planes[3 * QUAD : P, :], 0)
         nc.vector.memset(warm_in[:], 0.0)
-        nc.vector.memset(scale_win[0:96, :], 0)
+        nc.vector.memset(scale_win[0:SCALE_ROW0, :], 0)
+
         nc.sync.dma_start(offsets[:], offs)
-        nc.scalar.dma_start(scale_win[96:128, :], rows)
+        nc.scalar.dma_start(scale_win[SCALE_ROW0:P, :], tab_scales.rearrange("a q t -> (a q) t").bitcast(I32))
         nc.sync.dma_start(word_win[1][:], words(1))
-        nc.scalar.dma_start(ts_cols[:], ts[0].rearrange("(p c) -> p c", c=16))
+        nc.scalar.dma_start(ts_cols[:], ts[0].rearrange("(p c) -> p c", c=TS_COLS))
         make_identity(nc, ident[:], nomemset=True)
+        w4_rows = w4_scales[0].bitcast(I32)
         for quad in range(4):
-            nc.scalar.dma_start(planes[32 * quad : 32 * quad + 4, S // 4 :], w4_rows[4 * quad : 4 * quad + 4, :])
+            nc.scalar.dma_start(w4_plane[QUAD * quad : QUAD * quad + 4, :], w4_rows[4 * quad : 4 * quad + 4, :])
         nc.scalar.activation(warm_out[:], warm_in[:], SILU)
         nc.sync.dma_start(w8_raw[:], w8.rearrange("(p j) n -> p j n", j=4))
         nc.sync.dma_start(word_win[0][:], words(0))
         nc.sync.dma_start(w4_codes[:], w4_words[0].bitcast(I32))
-        for quarter in range(4):
-            for c in range(4):
-                col = 4 * quarter + c
-                nc.tensor.transpose(spread[quarter][:, c, :], ts_cols[:, col : col + 1].to_broadcast([P, P]), ident[:])
-            nc.scalar.copy(
-                ts_win[:].rearrange("q (p c) -> q p c", c=16)[:, :, 4 * quarter : 4 * quarter + 4],
-                spread[quarter][:].rearrange("q c p -> q p c"))
 
-        def slots(lo, hi):
-            return offsets[:, lo // 16 : hi // 16]
-
-        def gather_words(dst, a, lo, hi):
-            nc.vector.tensor_copy(dst, word_win[a][:].bitcast(U32).indirect(slots(lo, hi)))
+        ts_view = ts_win[:].rearrange("q (p c) -> q p c", c=TS_COLS)
+        for bank, turned in enumerate(spread):
+            for c in range(TURNS):
+                col = TURNS * bank + c
+                nc.tensor.transpose(turned[:, c, :], ts_cols[:, col : col + 1].to_broadcast([P, P]), ident[:])
+            nc.scalar.copy(ts_view[:, :, TURNS * bank : TURNS * (bank + 1)], turned[:].rearrange("q c p -> q p c"))
 
         nc.vector.tensor_copy(got_scales[:], scale_win[:].bitcast(U8).indirect(offsets[:]))
-        for first, row, count in ((0, 112, 4), (4, 88, 32), (36, 92, 32), (68, 96, 32), (108, 108, 4)):
-            nc.sync.dma_start(planes[first : first + count, 0 : S // 4], got_scales[row : row + count, :].bitcast(I32))
+        for first, row, count in plane_moves():
+            nc.sync.dma_start(table_planes[first : first + count, :], got_scales[row : row + count, :].bitcast(I32))
         nc.sync.dma_start(bias[:], b.rearrange("(p o) -> p o", o=1))
-        gather_words(got_words1[:], 1, 0, S)
-        plane_bytes = planes[:].bitcast(U8)
+        nc.vector.tensor_copy(got_words1[:], word_win[1][:].bitcast(U32).indirect(entries(0, S)))
+
         nc.scalar.copy(w8_bf[:], w8_raw[:].rearrange("p j n -> p n j"))
         nc.vector.quantize_mx(w8_codes[:].bitcast(FP8X4), w8_plane[:], w8_bf[:].rearrange("p n j -> p (n j)"))
-        for h in range(4):
-            got = keep.tile([P, 256], U32, name="got_words0_%d" % h, align_bytes=64)
-            cols = slice(256 * h, 256 * (h + 1))
-            gather_words(got[:], 0, 256 * h, 256 * (h + 1))
-            for g in range(2):
-                half = slice(256 * h + 128 * g, 256 * h + 128 * (g + 1))
+
+        plane_bytes = plane_tile[:].bitcast(U8)
+        for h, bank_sum in enumerate(acc):
+            cols = slice(BANK * h, BANK * (h + 1))
+            got_words0 = keep.tile([P, BANK], U32, name="got_words0_%d" % h, align_bytes=64)
+            nc.vector.tensor_copy(got_words0[:], word_win[0][:].bitcast(U32).indirect(entries(cols.start, cols.stop)))
+            for lo in range(0, BANK, E2M1_COLS):
+                part = slice(cols.start + lo, cols.start + lo + E2M1_COLS)
                 nc.tensor.matmul_mx(
-                    acc[h][:, 128 * g : 128 * (g + 1)],
+                    bank_sum[:, lo : lo + E2M1_COLS],
                     lhsT=w4_codes[:].bitcast(U8).bitcast(FP4X4), lhsT_scale=w4_plane.bitcast(U8),
-                    rhs=got_words1[:, half].bitcast(FP8X4), rhs_scale=plane_bytes[:, half], start=(g == 0), stop=False)
+                    rhs=got_words1[:, part].bitcast(FP8X4), rhs_scale=plane_bytes[:, part], start=(lo == 0), stop=False)
             nc.tensor.matmul_mx(
-                acc[h][:], lhsT=w8_codes[:].bitcast(FP8X4), lhsT_scale=w8_plane[:],
-                rhs=got[:].bitcast(FP8X4), rhs_scale=plane_bytes[12:P, cols], start=False, stop=True)
-            nc.scalar.copy(y[:, cols], acc[h][:])
-        for lo, hi in ((0, 256), (256, 512), (512, 768), (768, 896), (896, 1024)):
-            nc.vector.tensor_tensor(scaled[:, lo:hi], ts_win[:].indirect(slots(lo, hi)), y[:, lo:hi], MULT)
+                bank_sum[:], lhsT=w8_codes[:].bitcast(FP8X4), lhsT_scale=w8_plane[:],
+                rhs=got_words0[:].bitcast(FP8X4), rhs_scale=plane_bytes[PASS0_FIRST:P, cols], start=False, stop=True)
+            nc.scalar.copy(sums[:, cols], bank_sum[:])
+
+        for lo, hi in SLICES:
+            nc.vector.tensor_tensor(scaled[:, lo:hi], ts_win[:].indirect(entries(lo, hi)), sums[:, lo:hi], MULT)
             nc.scalar.activation(result[:, lo:hi], scaled[:, lo:hi], SILU, bias=bias[:])
             nc.sync.dma_start(out[:, lo:hi], result[:, lo:hi])

@@ -86,14 +86,14 @@ def tile_list_tabts_silu_kernel(tc, tab_words, tab_scales, w8, w4_words, w4_scal
         def entries(lo, hi):
             return offsets[:, lo // LIST_ROWS : hi // LIST_ROWS]
 
-        nc.vector.memset(ident[:], 0.0)
         nc.vector.memset(w4_plane, 0)
-        nc.vector.memset(table_planes[3 * QUAD : P, :], 0)
-        nc.vector.memset(warm_in[:], 0.0)
         nc.vector.memset(scale_win[0:SCALE_ROW0, :], 0)
+        nc.vector.memset(ident[:], 0.0)
+        nc.vector.memset(table_planes[3 * QUAD : P, :], 0)
+        nc.vector.tensor_copy(warm_in[:], ident[:, 0:1])
 
-        nc.sync.dma_start(offsets[:], offs)
         nc.scalar.dma_start(scale_win[SCALE_ROW0:P, :], tab_scales.rearrange("a q t -> (a q) t").bitcast(I32))
+        nc.sync.dma_start(offsets[:], offs)
         nc.sync.dma_start(word_win[1][:], words(1))
         nc.scalar.dma_start(ts_cols[:], ts[0].rearrange("(p c) -> p c", c=TS_COLS))
         make_identity(nc, ident[:], nomemset=True)

from contextlib import ExitStack

import concourse.mybir as mybir
from concourse.masks import make_identity

K, M, T, S = 1024, 128, 2048, 1024
FLOPS = 2 * K * M * S

F32 = mybir.dt.float32
BF16 = mybir.dt.bfloat16
I32 = mybir.dt.int32
U32 = mybir.dt.uint32
U16 = mybir.dt.uint16
U8 = mybir.dt.uint8
FP8X4 = mybir.dt.float8_e4m3fn_x4
FP4X4 = mybir.dt.float4_e2m1fn_x4
SILU = mybir.ActivationFunctionType.Silu
MULT = mybir.AluOpType.mult

P = 128
QUAD = 32
LIST_ROWS = 16
BLOCKS = 16
PLANE_WORDS = S // 4
W4_PLANE_WORDS = M // 4

SCALE_ROW0 = P - 2 * BLOCKS
PASS0_FIRST = 12

BANK = 256
E2M1_COLS = 128
SLICES = [(lo, lo + BANK) for lo in range(0, S - BANK, BANK)] + [(S - BANK, S - BANK // 2), (S - BANK // 2, S)]

TS_COLS = T // P
TURNS = 4


def place(stretch, lane):
    return (46 + 64 * stretch + 8 * lane) * 1024


def plane_moves():
    moves = [(0, SCALE_ROW0 + BLOCKS, 4)]
    for quad in range(3):
        first = QUAD * quad + 4
        moves.append((first, SCALE_ROW0 + 4 * quad - (PASS0_FIRST - 4), QUAD))
    moves.append((QUAD * 3 + PASS0_FIRST, SCALE_ROW0 + 4 * 3, 4))
    return moves


def tile_list_tabts_silu_kernel(tc, tab_words, tab_scales, w8, w4_words, w4_scales, ts, b, offs, out):
    nc = tc.nc
    with ExitStack() as ctx:
        keep = ctx.enter_context(tc.tile_pool(name="keep", bufs=1))
        far = ctx.enter_context(tc.tile_pool(name="far", bufs=1))
        psum = ctx.enter_context(tc.psum_pool(name="psum", bufs=1))

        offsets = keep.tile([P, S // LIST_ROWS], U16, name="offsets")
        scale_win = far.tile([P, T // 4], I32, name="scale_win", align_bytes=64, offset=place(0, 2))
        word_win = [far.tile([P, T], I32, name="word_win%d" % a, align_bytes=64, offset=place(a, 1 - a)) for a in range(2)]
        ts_win = far.tile([P, T], F32, name="ts_win", align_bytes=64, offset=place(2, 2))
        ts_cols = keep.tile([P, TS_COLS], F32, name="ts_cols", align_bytes=64)
        ident = keep.tile([P, P], F32, name="ident", align_bytes=64)
        w4_codes = keep.tile([P, 2 * M // 4], I32, name="w4_codes", align_bytes=64)
        w8_raw = far.tile([P, 4, M], F32, name="w8_raw", align_bytes=64, offset=place(2, 0))
        w8_bf = keep.tile([P, M, 4], BF16, name="w8_bf", align_bytes=64)
        w8_codes = keep.tile([P, M], U32, name="w8_codes", align_bytes=64)
        w8_plane = keep.tile([P, M], U8, name="w8_plane", align_bytes=64)
        bias = keep.tile([P, 1], F32, name="bias")
        warm_in = keep.tile([P, 1], F32, name="warm_in")
        warm_out = keep.tile([P, 1], F32, name="warm_out")
        got_scales = keep.tile([P, S], U8, name="got_scales", align_bytes=64)
        plane_tile = keep.tile([P, PLANE_WORDS + W4_PLANE_WORDS], I32, name="planes", align_bytes=64)
        table_planes = plane_tile[:, 0:PLANE_WORDS]
        w4_plane = plane_tile[:, PLANE_WORDS:]
        got_words1 = keep.tile([P, S], U32, name="got_words1", align_bytes=64)
        sums = keep.tile([P, S], F32, name="y", align_bytes=64)
        scaled = far.tile([P, S], F32, name="scaled", align_bytes=64, offset=place(1, 1))
        result = far.tile([P, S], F32, name="result", align_bytes=64, offset=place(0, 0))
        acc = [psum.tile([P, BANK], F32, name="acc%d" % h) for h in range(S // BANK)]
        spread = [psum.tile([P, TURNS, P], F32, name="spread%d" % h) for h in range(TS_COLS // TURNS)]

        def words(a):
            return tab_words[a].rearrange("p t i -> p (t i)").bitcast(I32)

        def entries(lo, hi):
            return offsets[:, lo // LIST_ROWS : hi // LIST_ROWS]

        nc.vector.memset(w4_plane, 0)
        nc.vector.memset(scale_win[0:SCALE_ROW0, :], 0)
        nc.vector.memset(ident[:], 0.0)
        nc.vector.memset(table_planes[3 * QUAD : P, :], 0)
        nc.vector.tensor_copy(warm_in[:], ident[:, 0:1])

        nc.scalar.dma_start(scale_win[SCALE_ROW0:P, :], tab_scales.rearrange("a q t -> (a q) t").bitcast(I32))
        nc.sync.dma_start(offsets[:], offs)
        nc.sync.dma_start(word_win[1][:], words(1))
        nc.scalar.dma_start(ts_cols[:], ts[0].rearrange("(p c) -> p c", c=TS_COLS))
        make_identity(nc, ident[:], nomemset=True)
        w4_rows = w4_scales[0].bitcast(I32)
        for quad in range(4):
            nc.scalar.dma_start(w4_plane[QUAD * quad : QUAD * quad + 4, :], w4_rows[4 * quad : 4 * quad + 4, :])
        nc.scalar.activation(warm_out[:], warm_in[:], SILU)
        nc.sync.dma_start(w8_raw[:], w8.rearrange("(p j) n -> p j n", j=4))
        nc.sync.dma_start(word_win[0][:], words(0))
        nc.sync.dma_start(w4_codes[:], w4_words[0].bitcast(I32))

        ts_view = ts_win[:].rearrange("q (p c) -> q p c", c=TS_COLS)
        for bank, turned in enumerate(spread):
            for c in range(TURNS):
                col = TURNS * bank + c
                nc.tensor.transpose(turned[:, c, :], ts_cols[:, col : col + 1].to_broadcast([P, P]), ident[:])
            nc.scalar.copy(ts_view[:, :, TURNS * bank : TURNS * (bank + 1)], turned[:].rearrange("q c p -> q p c"))

        nc.vector.tensor_copy(got_scales[:], scale_win[:].bitcast(U8).indirect(offsets[:]))
        for first, row, count in plane_moves():
            nc.sync.dma_start(table_planes[first : first + count, :], got_scales[row : row + count, :].bitcast(I32))
        nc.sync.dma_start(bias[:], b.rearrange("(p o) -> p o", o=1))
        nc.vector.tensor_copy(got_words1[:], word_win[1][:].bitcast(U32).indirect(entries(0, S)))

        nc.scalar.copy(w8_bf[:], w8_raw[:].rearrange("p j n -> p n j"))
        nc.vector.quantize_mx(w8_codes[:].bitcast(FP8X4), w8_plane[:], w8_bf[:].rearrange("p n j -> p (n j)"))

        plane_bytes = plane_tile[:].bitcast(U8)
        for h, bank_sum in enumerate(acc):
            cols = slice(BANK * h, BANK * (h + 1))
            got_words0 = keep.tile([P, BANK], U32, name="got_words0_%d" % h, align_bytes=64)
            nc.vector.tensor_copy(got_words0[:], word_win[0][:].bitcast(U32).indirect(entries(cols.start, cols.stop)))
            for lo in range(0, BANK, E2M1_COLS):
                part = slice(cols.start + lo, cols.start + lo + E2M1_COLS)
                nc.tensor.matmul_mx(
                    bank_sum[:, lo : lo + E2M1_COLS],
                    lhsT=w4_codes[:].bitcast(U8).bitcast(FP4X4), lhsT_scale=w4_plane.bitcast(U8),
                    rhs=got_words1[:, part].bitcast(FP8X4), rhs_scale=plane_bytes[:, part], start=(lo == 0), stop=False)
            nc.tensor.matmul_mx(
                bank_sum[:], lhsT=w8_codes[:].bitcast(FP8X4), lhsT_scale=w8_plane[:],
                rhs=got_words0[:].bitcast(FP8X4), rhs_scale=plane_bytes[PASS0_FIRST:P, cols], start=False, stop=True)
            nc.scalar.copy(sums[:, cols], bank_sum[:])

        for lo, hi in SLICES:
            nc.vector.tensor_tensor(scaled[:, lo:hi], ts_win[:].indirect(entries(lo, hi)), sums[:, lo:hi], MULT)
            nc.scalar.activation(result[:, lo:hi], scaled[:, lo:hi], SILU, bias=bias[:])
            nc.sync.dma_start(out[:, lo:hi], result[:, lo:hi])
